import numpy as np
import ml_dtypes


def mxq(x, axis, fmt="e4m3"):
    dtype, down = {"e4m3": (ml_dtypes.float8_e4m3fn, 7), "e5m2": (ml_dtypes.float8_e5m2, 14)}[fmt]
    v = np.moveaxis(np.asarray(x, np.float32).astype(ml_dtypes.bfloat16).astype(np.float64), axis, -1)
    blocks = v.reshape(v.shape[:-1] + (-1, 32))
    amax = np.abs(blocks).max(-1, keepdims=True)
    byte = np.maximum(np.where(amax > 0, np.frexp(amax)[1] - 1 + 127, 0) - down, 1)
    scale = np.exp2(byte - 127.0)
    codes = (blocks / scale).astype(np.float32).astype(dtype).astype(np.float64)
    return np.moveaxis((codes * scale).reshape(v.shape), -1, axis)


WIDE = False


def mx_kscale(k):
    if not WIDE:
        return np.ones(k)
    levels = np.array([10, -10, 5, -5, 0])
    if k % 512:
        return np.exp2(np.random.permutation(np.resize(levels, k // 32))).repeat(32)
    a = np.empty((k // 512, 16))
    for p in range(k // 512):
        a[p, :8] = np.random.permutation(np.resize(levels, 8))
        for g in range(8):
            far = levels[np.abs(levels - a[p, g]) >= 10]
            a[p, g + 8] = far[np.random.randint(len(far))]
    return np.exp2(a.ravel()).repeat(32)


def f64(x):
    return np.asarray(x).astype(np.float64)


def striped(idx):
    return np.tile(np.asarray(idx).reshape(-1, 16).T, (8, 1)).astype(np.uint16)


def unstriped(offs):
    return offs[:16].T.reshape(-1).astype(np.int64)


E2M1 = np.array([0.0, 0.5, 1.0, 1.5, 2.0, 3.0, 4.0, 6.0, -0.0, -0.5, -1.0, -1.5, -2.0, -3.0, -4.0, -6.0])


def pack_weight(w, fmt):
    k, n = w.shape
    w = f64(np.asarray(w, np.float32).astype(ml_dtypes.bfloat16)).reshape(k // 32, 32, n)
    amax = np.abs(w).max(1)
    if fmt == "e4m3":
        byte = np.frexp(amax)[1] - 1 + 127 - 7
    else:
        mant, ex = np.frexp(amax / 6.0)
        byte = np.where(mant > 0.5, ex, ex - 1) + 127
    byte = np.clip(np.where(amax > 0, byte, 1), 1, 254)
    scaled = (w * np.exp2(127.0 - byte)[:, None, :]).reshape(k, n).astype(np.float32)
    by_word = np.ascontiguousarray(scaled.reshape(k // 512, 128, 4, n).transpose(0, 1, 3, 2))
    if fmt == "e4m3":
        words = by_word.astype(ml_dtypes.float8_e4m3fn).view(np.uint8)
    else:
        c = by_word.astype(ml_dtypes.float4_e2m1fn).view(np.uint8) & 0xF
        words = (c[..., 0::2] | (c[..., 1::2] << 4)).reshape(k // 512, 128, 2 * n)
    return np.ascontiguousarray(words), np.ascontiguousarray(byte.astype(np.uint8).reshape(k // 512, 16, n))


def unpack_weight(words, scales, fmt):
    g, _, n = scales.shape
    words = np.ascontiguousarray(words).reshape(g, 128, n, -1)
    if fmt == "e4m3":
        vals = words.view(ml_dtypes.float8_e4m3fn).astype(np.float64)
    else:
        nib = np.empty((g, 128, n, 4), np.uint8)
        nib[..., 0::2] = words & 0xF
        nib[..., 1::2] = words >> 4
        vals = E2M1[nib]
    vals = vals * np.repeat(np.exp2(scales.astype(np.float64) - 127.0), 8, axis=1)[..., None]
    return vals.transpose(0, 1, 3, 2).reshape(g * 512, n)


def softplus(v):
    return np.log(1.0 + np.exp(v))


def bf(x):
    return np.asarray(x, np.float32).astype(ml_dtypes.bfloat16)


def planes(Y):
    r, m = Y.shape
    b = f64(bf(Y)).reshape(r // 32, 32, m)
    amax = np.abs(b).max(1)
    byte = np.clip(np.where(amax > 0, np.frexp(amax)[1] - 1 + 127 - 7, 1), 1, 254)
    codes = (b * np.exp2(127.0 - byte)[:, None, :]).reshape(r, m).astype(np.float32).astype(ml_dtypes.float8_e4m3fn).view(np.uint8)
    words = codes.reshape(r // 512, 128, 4, m).transpose(0, 1, 3, 2)
    return np.ascontiguousarray(words), np.ascontiguousarray(byte.astype(np.uint8).reshape(r // 512, 16, m))


K, T, J, L, N = 512, 2048, 512, 512, 512


def setup_inputs():
    n = np.random.standard_normal
    idx = np.random.permutation(T)[:J]
    fk = mx_kscale(K)
    fl = mx_kscale(L)
    xtp = pack_weight(n((K, T)) / fk[:, None], "e2m1")
    wap = pack_weight(n((K, N)) * 1 / np.sqrt(K) * fk[:, None], "e4m3")
    sxp = pack_weight(n((L, J)) / fl[:, None], "e2m1")
    wbp = pack_weight(n((L, N)) * 1 / np.sqrt(L) * fl[:, None], "e4m3")
    vbp = pack_weight(n((L, N)) * 1 / np.sqrt(L) * fl[:, None], "e2m1")
    return {
        "xt_words": xtp[0],
        "xt_scales": xtp[1],
        "wa_words": wap[0],
        "wa_scales": wap[1],
        "va": (n((K, N)) * 1 / np.sqrt(K) * fk[:, None]).astype(np.float32),
        "sx_words": sxp[0],
        "sx_scales": sxp[1],
        "wb_words": wbp[0],
        "wb_scales": wbp[1],
        "vb_words": vbp[0],
        "vb_scales": vbp[1],
        "offs": striped(idx),
    }


def reference(xt_words, xt_scales, wa_words, wa_scales, va, sx_words, sx_scales, wb_words, wb_scales, vb_words, vb_scales, offs):
    idx = unstriped(offs)
    xtu = unpack_weight(xt_words, xt_scales, "e2m1")
    wau = unpack_weight(wa_words, wa_scales, "e4m3")
    sxu = unpack_weight(sx_words, sx_scales, "e2m1")
    wbu = unpack_weight(wb_words, wb_scales, "e4m3")
    vbu = unpack_weight(vb_words, vb_scales, "e2m1")
    xtidxg = xtu[:, idx]
    a = wau.T @ xtidxg
    vaq = mxq(f64(va), 0, "e4m3")
    u = vaq.T @ xtidxg
    b = wbu.T @ sxu
    v = vbu.T @ sxu
    pa = softplus(u)
    pb = softplus(v)
    y = (pa * a + pb * b) / (pa + pb + 0.1)
    words, scales = planes(y)
    return y, words, scales

@@ -1,0 +1,234 @@
+from contextlib import ExitStack
+
+import concourse.mybir as mybir
+
+K, T, J, N = 512, 2048, 512, 512
+FLOPS = 4 * 2 * K * J * N
+
+F32 = mybir.dt.float32
+BF16 = mybir.dt.bfloat16
+I32 = mybir.dt.int32
+U16 = mybir.dt.uint16
+U8 = mybir.dt.uint8
+FP8X4 = mybir.dt.float8_e4m3fn_x4
+FP4X4 = mybir.dt.float4_e2m1fn_x4
+ALU = mybir.AluOpType
+ACT = mybir.ActivationFunctionType
+
+P = 128
+PACK = 4
+QUADS = 4
+M = N // PACK
+CHUNKS = 4
+C = J // CHUNKS
+LINEAR_FROM = 30.0
+
+
+def tile_list_precision_weighted_pair_pl_kernel(
+    tc, xt_words, xt_scales, wa_words, wa_scales, va, sx_words, sx_scales,
+    wb_words, wb_scales, vb_words, vb_scales, offs, out_0, out_1, out_2,
+):
+    nc = tc.nc
+    with ExitStack() as ctx:
+        sb = ctx.enter_context(tc.tile_pool(name="sb", bufs=1))
+        ps = ctx.enter_context(tc.psum_pool(name="ps", bufs=1))
+
+        def tile(name, shape, dtype, tag=None):
+            return sb.tile(shape, dtype, name=name, tag=tag or name, align_bytes=64)
+
+        def load_scales(plane, scales, queue):
+            for q in range(QUADS):
+                queue.dma_start(
+                    out=plane[32 * q : 32 * q + 4, :].bitcast(I32),
+                    in_=scales[0, 4 * q : 4 * q + 4, :].bitcast(I32),
+                )
+
+        def words_of(words):
+            return words[0].rearrange("p n t -> p (n t)").bitcast(I32)
+
+        offsets = sb.tile([P, J // 16], U16, name="offsets")
+        nc.sync.dma_start(offsets[:], offs)
+
+        xt_plane = tile("xt_plane", [P, T], U8)
+        nc.gpsimd.memset(xt_plane[:].bitcast(I32), 0)
+        load_scales(xt_plane, xt_scales, nc.sync)
+
+        va_rows = va.rearrange("(p j) n -> p j n", j=PACK)
+        va_raw = [tile("va_raw%d" % h, [P, PACK, N // 2], F32) for h in range(2)]
+        nc.sync.dma_start(out=va_raw[0][:], in_=va_rows[:, :, : N // 2])
+        xt_table = tile("xt_table", [P, T], U16, tag="packed_raw")
+        nc.sync.dma_start(out=xt_table[:].bitcast(I32), in_=xt_words[0].bitcast(I32))
+        nc.sync.dma_start(out=va_raw[1][:], in_=va_rows[:, :, N // 2 :])
+
+        warm = tile("warm", [P, 1], F32)
+        nc.vector.memset(warm[:], 0.0)
+        sx_plane = tile("sx_plane", [P, J], U8)
+        vb_plane_raw = tile("vb_plane_raw", [P, N], U8)
+        nc.gpsimd.memset(vb_plane_raw[:].bitcast(I32), 0)
+        nc.gpsimd.memset(sx_plane[:].bitcast(I32), 0)
+        warm_out = tile("warm_out", [P, 1], F32)
+        nc.scalar.activation(warm_out[:], warm[:], ACT.Exp)
+        load_scales(vb_plane_raw, vb_scales, nc.sync)
+        load_scales(sx_plane, sx_scales, nc.sync)
+        sx_codes = tile("sx_codes", [P, 2 * J], U8)
+        vb_raw = tile("vb_raw", [P, 2 * N], U8)
+        nc.gpsimd.dma_start(out=vb_raw[:].bitcast(I32), in_=vb_words[0].bitcast(I32))
+        nc.gpsimd.dma_start(out=sx_codes[:].bitcast(I32), in_=sx_words[0].bitcast(I32))
+
+        w_plane_raw = tile("w_plane_raw", [P, 2 * N], U8)
+        nc.gpsimd.memset(w_plane_raw[:].bitcast(I32), 0)
+
+        xg_plane = tile("xg_plane", [P, J], U8)
+        xg_codes = tile("xg_codes", [P, J], U16)
+        nc.vector.tensor_copy(xg_plane[:], xt_plane[:].indirect(offsets[:]))
+        nc.vector.tensor_copy(xg_codes[:], xt_table[:].indirect(offsets[:]))
+
+        va_bf = tile("va_bf", [P, PACK, M, PACK], BF16)
+        for h in range(2):
+            dst = va_bf[:, :, h * M // 2 : (h + 1) * M // 2, :].rearrange("p t m j -> p m j t")
+            src = va_raw[h][:].rearrange("p j (m t) -> p m j t", t=PACK)
+            if h == 0:
+                nc.scalar.copy(dst, src)
+            else:
+                nc.vector.tensor_copy(dst, src)
+        va_codes = tile("va_codes", [P, N], I32)
+        va_plane = tile("va_plane", [P, N], U8)
+        banks = {}
+
+        def bank(i, name):
+            return ps.tile([P, 512], F32, name=name, tag="bank%d" % i)
+
+        grown = tile("grown", [P, PACK, 2, J], F32)
+        for t in range(PACK):
+            cols = slice(t * M, (t + 1) * M)
+            nc.vector.quantize_mx(
+                out=va_codes[:, cols].bitcast(FP8X4),
+                scales=va_plane[:, cols],
+                in_=va_bf[:, t, :, :].rearrange("p m j -> p (m j)"),
+            )
+            banks["u", t] = bank(t, "u%d" % t)
+            nc.tensor.matmul_mx(
+                out=banks["u", t][:],
+                lhsT=va_codes[:, cols].bitcast(FP8X4), lhsT_scale=va_plane[:, cols],
+                rhs=xg_codes[:].bitcast(FP4X4), rhs_scale=xg_plane[:],
+                start=True, stop=True,
+            )
+            nc.scalar.activation(grown[:, t, 0, :], banks["u", t][:], ACT.Exp)
+
+        vb_codes = tile("vb_codes", [P, 2 * N], U8)
+        vb_plane = tile("vb_plane", [P, N], U8)
+        nc.vector.tensor_copy(
+            vb_codes[:].rearrange("p (t m b) -> p m t b", t=PACK, b=2),
+            vb_raw[:].rearrange("p (m t b) -> p m t b", t=PACK, b=2),
+        )
+        nc.vector.tensor_copy(
+            vb_plane[:].rearrange("p (t m) -> p m t", t=PACK),
+            vb_plane_raw[:].rearrange("p (m t) -> p m t", t=PACK),
+        )
+        for t in range(PACK):
+            banks["v", t] = bank(PACK + t, "v%d" % t)
+            nc.tensor.matmul_mx(
+                out=banks["v", t][:],
+                lhsT=vb_codes[:, 2 * t * M : 2 * (t + 1) * M].bitcast(FP4X4),
+                lhsT_scale=vb_plane[:, t * M : (t + 1) * M],
+                rhs=sx_codes[:].bitcast(FP4X4), rhs_scale=sx_plane[:],
+                start=True, stop=True,
+            )
+            nc.scalar.activation(grown[:, t, 1, :], banks["v", t][:], ACT.Exp)
+
+        w_raw = tile("w_raw", [P, 2 * N], I32, tag="packed_raw")
+        nc.sync.dma_start(out=w_raw[:, :N], in_=words_of(wa_words))
+        nc.sync.dma_start(out=w_raw[:, N:], in_=words_of(wb_words))
+        load_scales(w_plane_raw[:, :N], wa_scales, nc.sync)
+        load_scales(w_plane_raw[:, N:], wb_scales, nc.sync)
+        w_codes = tile("w_codes", [P, 2 * N], I32)
+        w_plane = tile("w_plane", [P, 2 * N], U8)
+        nc.vector.tensor_copy(
+            w_plane[:].rearrange("p (w t m) -> p w m t", w=2, t=PACK),
+            w_plane_raw[:].rearrange("p (w m t) -> p w m t", w=2, t=PACK),
+        )
+        nc.vector.tensor_copy(
+            w_codes[:].rearrange("p (w t m) -> p w m t", w=2, t=PACK),
+            w_raw[:].rearrange("p (w m t) -> p w m t", w=2, t=PACK),
+        )
+
+        logs = tile("logs", [P, PACK, 2, J], F32)
+        prec = tile("prec", [P, 2, PACK, J], F32)
+        total = tile("total", [P, PACK, J], F32)
+        log_total = tile("log_total", [P, PACK, J], F32)
+        for t in range(PACK):
+            nc.scalar.activation(
+                logs[:, t, :, :].rearrange("p s j -> p (s j)"),
+                grown[:, t, :, :].rearrange("p s j -> p (s j)"), ACT.Ln, bias=1.0,
+            )
+            for s, side in enumerate("uv"):
+                nc.vector.scalar_tensor_tensor(
+                    prec[:, s, t, :], logs[:, t, s, :], LINEAR_FROM, banks[side, t][:],
+                    ALU.min, ALU.max,
+                )
+            nc.gpsimd.tensor_tensor(total[:, t, :], prec[:, 0, t, :], prec[:, 1, t, :], ALU.add)
+        for t in range(PACK):
+            nc.scalar.activation(log_total[:, t, :], total[:, t, :], ACT.Ln, bias=0.1)
+
+        terms = tile("terms", [P, CHUNKS, 2, PACK * C], F32)
+        numer = tile("numer", [P, CHUNKS, PACK * C], F32)
+        moving = ((xg_codes[:].bitcast(U8), xg_plane), (sx_codes[:], sx_plane))
+        for c in range(CHUNKS):
+            js = slice(c * C, (c + 1) * C)
+            for s in range(2):
+                est = bank(s * PACK + c, "est%d_%d" % (s, c))
+                codes, plane = moving[s]
+                for t in range(PACK):
+                    cols = slice(s * N + t * M, s * N + (t + 1) * M)
+                    nc.tensor.matmul_mx(
+                        out=est[:, t * C : (t + 1) * C],
+                        lhsT=w_codes[:, cols].bitcast(FP8X4), lhsT_scale=w_plane[:, cols],
+                        rhs=codes[:, 2 * c * C : 2 * (c + 1) * C].bitcast(FP4X4),
+                        rhs_scale=plane[:, js],
+                        start=True, stop=True,
+                    )
+                nc.vector.tensor_tensor(
+                    terms[:, c, s, :].rearrange("p (t j) -> p t j", t=PACK),
+                    prec[:, s, :, js],
+                    est[:].rearrange("p (t j) -> p t j", t=PACK), ALU.mult,
+                )
+            adder = nc.vector if c == CHUNKS - 1 else nc.gpsimd
+            adder.tensor_tensor(numer[:, c, :], terms[:, c, 0, :], terms[:, c, 1, :], ALU.add)
+
+        recip = tile("recip", [P, CHUNKS, PACK * C], F32)
+        y = tile("y", [P, CHUNKS, PACK * C], F32)
+        y_bf = tile("y_bf", [P, CHUNKS, C * PACK], BF16)
+        y_codes = tile("y_codes", [P, J], I32)
+        y_plane = tile("y_plane", [P, J], U8)
+        out_rows = out_0.rearrange("(p t) j -> p t j", t=PACK)
+        for c in range(CHUNKS):
+            js = slice(c * C, (c + 1) * C)
+            nc.scalar.activation(
+                recip[:, c, :].rearrange("p (t j) -> p t j", t=PACK),
+                log_total[:, :, js], ACT.Exp, scale=-1.0,
+            )
+        for c in range(CHUNKS):
+            js = slice(c * C, (c + 1) * C)
+            nc.vector.tensor_tensor(y[:, c, :], numer[:, c, :], recip[:, c, :], ALU.mult)
+            nc.sync.dma_start(
+                out=out_rows[:, :, js], in_=y[:, c, :].rearrange("p (t j) -> p t j", t=PACK)
+            )
+        for c in range(CHUNKS):
+            js = slice(c * C, (c + 1) * C)
+            dst = y_bf[:, c, :].rearrange("p (g i t) -> p g t i", i=4, t=PACK)
+            src = y[:, c, :].rearrange("p (t g i) -> p g t i", i=4, t=PACK)
+            if c < 2:
+                nc.scalar.copy(dst, src)
+            else:
+                nc.vector.tensor_copy(dst, src)
+            nc.vector.quantize_mx(
+                out=y_codes[:, js].bitcast(FP8X4), scales=y_plane[:, js], in_=y_bf[:, c, :]
+            )
+        for h in range(2):
+            half = slice(h * J // 2, (h + 1) * J // 2)
+            nc.sync.dma_start(out=words_of(out_1)[:, half], in_=y_codes[:, half])
+        for q in range(QUADS):
+            nc.scalar.dma_start(
+                out=out_2[0, 4 * q : 4 * q + 4, :].bitcast(I32),
+                in_=y_plane[32 * q : 32 * q + 4, :].bitcast(I32),
+            )

@@ -21,7 +21,9 @@ QUADS = 4
 M = N // PACK
 CHUNKS = 4
 C = J // CHUNKS
+H = J // 2
 LINEAR_FROM = 30.0
+SCALAR_M = 40
 
 
 def tile_list_precision_weighted_pair_pl_kernel(
@@ -48,73 +50,43 @@ def tile_list_precision_weighted_pair_pl_kernel(
 
         offsets = sb.tile([P, J // 16], U16, name="offsets")
         nc.sync.dma_start(offsets[:], offs)
-
-        xt_plane = tile("xt_plane", [P, T], U8)
-        nc.gpsimd.memset(xt_plane[:].bitcast(I32), 0)
-        load_scales(xt_plane, xt_scales, nc.sync)
-
-        va_rows = va.rearrange("(p j) n -> p j n", j=PACK)
-        va_raw = [tile("va_raw%d" % h, [P, PACK, N // 2], F32) for h in range(2)]
-        nc.sync.dma_start(out=va_raw[0][:], in_=va_rows[:, :, : N // 2])
-        xt_table = tile("xt_table", [P, T], U16, tag="packed_raw")
+        xt_table = tile("xt_table", [P, T], U16)
         nc.sync.dma_start(out=xt_table[:].bitcast(I32), in_=xt_words[0].bitcast(I32))
-        nc.sync.dma_start(out=va_raw[1][:], in_=va_rows[:, :, N // 2 :])
+        sx_codes = tile("sx_codes", [P, 2 * J], U8)
+        vb_raw = tile("vb_raw", [P, 2 * N], U8)
+        nc.sync.dma_start(out=vb_raw[:].bitcast(I32), in_=vb_words[0].bitcast(I32))
+        nc.sync.dma_start(out=sx_codes[:].bitcast(I32), in_=sx_words[0].bitcast(I32))
+
+        vb_plane_raw = tile("vb_plane_raw", [P, N], U8)
+        sx_plane = tile("sx_plane", [P, J], U8)
+        nc.gpsimd.memset(vb_plane_raw[:].bitcast(I32), 0)
+        nc.gpsimd.memset(sx_plane[:].bitcast(I32), 0)
+        load_scales(vb_plane_raw, vb_scales, nc.sync)
+        load_scales(sx_plane, sx_scales, nc.sync)
+        va_raw = tile("va_raw", [P, PACK, N], F32)
+        nc.gpsimd.dma_start(out=va_raw[:], in_=va.rearrange("(p j) n -> p j n", j=PACK))
 
         warm = tile("warm", [P, 1], F32)
         nc.vector.memset(warm[:], 0.0)
-        sx_plane = tile("sx_plane", [P, J], U8)
-        vb_plane_raw = tile("vb_plane_raw", [P, N], U8)
-        nc.gpsimd.memset(vb_plane_raw[:].bitcast(I32), 0)
-        nc.gpsimd.memset(sx_plane[:].bitcast(I32), 0)
         warm_out = tile("warm_out", [P, 1], F32)
         nc.scalar.activation(warm_out[:], warm[:], ACT.Exp)
-        load_scales(vb_plane_raw, vb_scales, nc.sync)
-        load_scales(sx_plane, sx_scales, nc.sync)
-        sx_codes = tile("sx_codes", [P, 2 * J], U8)
-        vb_raw = tile("vb_raw", [P, 2 * N], U8)
-        nc.gpsimd.dma_start(out=vb_raw[:].bitcast(I32), in_=vb_words[0].bitcast(I32))
-        nc.gpsimd.dma_start(out=sx_codes[:].bitcast(I32), in_=sx_words[0].bitcast(I32))
+        xt_plane = tile("xt_plane", [P, T], U8)
+        nc.vector.memset(xt_plane[:].bitcast(I32), 0)
+        load_scales(xt_plane, xt_scales, nc.sync)
 
-        w_plane_raw = tile("w_plane_raw", [P, 2 * N], U8)
-        nc.gpsimd.memset(w_plane_raw[:].bitcast(I32), 0)
+        w_packed = tile("w_packed", [P, 2 * N + 2 * N // PACK], I32)
+        w_raw = w_packed[:, : 2 * N]
+        nc.gpsimd.memset(w_packed[:, 2 * N :], 0)
+        w_plane_raw = w_packed[:, 2 * N :].bitcast(U8)
+        nc.gpsimd.dma_start(out=w_raw[:, :N], in_=words_of(wa_words))
+        nc.gpsimd.dma_start(out=w_raw[:, N:], in_=words_of(wb_words))
 
-        xg_plane = tile("xg_plane", [P, J], U8)
-        xg_codes = tile("xg_codes", [P, J], U16)
-        nc.vector.tensor_copy(xg_plane[:], xt_plane[:].indirect(offsets[:]))
-        nc.vector.tensor_copy(xg_codes[:], xt_table[:].indirect(offsets[:]))
-
-        va_bf = tile("va_bf", [P, PACK, M, PACK], BF16)
-        for h in range(2):
-            dst = va_bf[:, :, h * M // 2 : (h + 1) * M // 2, :].rearrange("p t m j -> p m j t")
-            src = va_raw[h][:].rearrange("p j (m t) -> p m j t", t=PACK)
-            if h == 0:
-                nc.scalar.copy(dst, src)
-            else:
-                nc.vector.tensor_copy(dst, src)
-        va_codes = tile("va_codes", [P, N], I32)
-        va_plane = tile("va_plane", [P, N], U8)
         banks = {}
 
         def bank(i, name):
             return ps.tile([P, 512], F32, name=name, tag="bank%d" % i)
 
         grown = tile("grown", [P, PACK, 2, J], F32)
-        for t in range(PACK):
-            cols = slice(t * M, (t + 1) * M)
-            nc.vector.quantize_mx(
-                out=va_codes[:, cols].bitcast(FP8X4),
-                scales=va_plane[:, cols],
-                in_=va_bf[:, t, :, :].rearrange("p m j -> p (m j)"),
-            )
-            banks["u", t] = bank(t, "u%d" % t)
-            nc.tensor.matmul_mx(
-                out=banks["u", t][:],
-                lhsT=va_codes[:, cols].bitcast(FP8X4), lhsT_scale=va_plane[:, cols],
-                rhs=xg_codes[:].bitcast(FP4X4), rhs_scale=xg_plane[:],
-                start=True, stop=True,
-            )
-            nc.scalar.activation(grown[:, t, 0, :], banks["u", t][:], ACT.Exp)
-
         vb_codes = tile("vb_codes", [P, 2 * N], U8)
         vb_plane = tile("vb_plane", [P, N], U8)
         nc.vector.tensor_copy(
@@ -136,32 +108,55 @@ def tile_list_precision_weighted_pair_pl_kernel(
             )
             nc.scalar.activation(grown[:, t, 1, :], banks["v", t][:], ACT.Exp)
 
-        w_raw = tile("w_raw", [P, 2 * N], I32, tag="packed_raw")
-        nc.sync.dma_start(out=w_raw[:, :N], in_=words_of(wa_words))
-        nc.sync.dma_start(out=w_raw[:, N:], in_=words_of(wb_words))
+
+        xg_plane = tile("xg_plane", [P, J], U8)
+        xg_codes = tile("xg_codes", [P, J], U16)
+        nc.vector.tensor_copy(xg_codes[:], xt_table[:].indirect(offsets[:]))
+        nc.vector.tensor_copy(xg_plane[:], xt_plane[:].indirect(offsets[:]))
+
+        va_bf = tile("va_bf", [P, PACK, M, PACK], BF16, tag="vb_plane_raw")
+        dealt = va_bf[:].rearrange("p t m j -> p m j t")
+        rows = va_raw[:].rearrange("p j (m t) -> p m j t", t=PACK)
+        nc.scalar.copy(dealt[:, :SCALAR_M], rows[:, :SCALAR_M])
+        nc.vector.tensor_copy(dealt[:, SCALAR_M:], rows[:, SCALAR_M:])
+        va_codes = tile("va_codes", [P, N], I32)
+        va_plane = tile("va_plane", [P, N], U8)
+        for t in range(PACK):
+            cols = slice(t * M, (t + 1) * M)
+            nc.vector.quantize_mx(
+                out=va_codes[:, cols].bitcast(FP8X4),
+                scales=va_plane[:, cols],
+                in_=va_bf[:, t, :, :].rearrange("p m j -> p (m j)"),
+            )
+            banks["u", t] = bank(t, "u%d" % t)
+            nc.tensor.matmul_mx(
+                out=banks["u", t][:],
+                lhsT=va_codes[:, cols].bitcast(FP8X4), lhsT_scale=va_plane[:, cols],
+                rhs=xg_codes[:].bitcast(FP4X4), rhs_scale=xg_plane[:],
+                start=True, stop=True,
+            )
+            nc.scalar.activation(grown[:, t, 0, :], banks["u", t][:], ACT.Exp)
+
         load_scales(w_plane_raw[:, :N], wa_scales, nc.sync)
         load_scales(w_plane_raw[:, N:], wb_scales, nc.sync)
-        w_codes = tile("w_codes", [P, 2 * N], I32)
-        w_plane = tile("w_plane", [P, 2 * N], U8)
+        w_codes = tile("w_codes", [P, 2 * N], I32, tag="vb_plane_raw")
+        w_plane = tile("w_plane", [P, 2 * N], U8, tag="va_plane")
         nc.vector.tensor_copy(
             w_plane[:].rearrange("p (w t m) -> p w m t", w=2, t=PACK),
-            w_plane_raw[:].rearrange("p (w m t) -> p w m t", w=2, t=PACK),
+            w_plane_raw.rearrange("p (w m t) -> p w m t", w=2, t=PACK),
         )
         nc.vector.tensor_copy(
             w_codes[:].rearrange("p (w t m) -> p w m t", w=2, t=PACK),
-            w_raw[:].rearrange("p (w m t) -> p w m t", w=2, t=PACK),
+            w_raw.rearrange("p (w m t) -> p w m t", w=2, t=PACK),
         )
 
-        logs = tile("logs", [P, PACK, 2, J], F32)
-        prec = tile("prec", [P, 2, PACK, J], F32)
+        logs = tile("logs", [P, PACK, 2, J], F32, tag="va_codes")
+        prec = tile("prec", [P, 2, PACK, J], F32, tag="w_packed")
         total = tile("total", [P, PACK, J], F32)
         log_total = tile("log_total", [P, PACK, J], F32)
         for t in range(PACK):
-            nc.scalar.activation(
-                logs[:, t, :, :].rearrange("p s j -> p (s j)"),
-                grown[:, t, :, :].rearrange("p s j -> p (s j)"), ACT.Ln, bias=1.0,
-            )
             for s, side in enumerate("uv"):
+                nc.scalar.activation(logs[:, t, s, :], grown[:, t, s, :], ACT.Ln, bias=1.0)
                 nc.vector.scalar_tensor_tensor(
                     prec[:, s, t, :], logs[:, t, s, :], LINEAR_FROM, banks[side, t][:],
                     ALU.min, ALU.max,
@@ -170,65 +165,67 @@ def tile_list_precision_weighted_pair_pl_kernel(
         for t in range(PACK):
             nc.scalar.activation(log_total[:, t, :], total[:, t, :], ACT.Ln, bias=0.1)
 
-        terms = tile("terms", [P, CHUNKS, 2, PACK * C], F32)
-        numer = tile("numer", [P, CHUNKS, PACK * C], F32)
-        moving = ((xg_codes[:].bitcast(U8), xg_plane), (sx_codes[:], sx_plane))
-        for c in range(CHUNKS):
-            js = slice(c * C, (c + 1) * C)
+        pieces = [(h, r) for h in range(2) for r in range(2)]
+
+        def piece_of(whole, h, r):
+            return whole[:, 2 * r : 2 * r + 2, h * H : (h + 1) * H]
+
+        def paired(flat):
+            return flat.rearrange("p (t j) -> p t j", t=2)
+
+        terms = tile("terms", [P, len(pieces), 2, 2 * H], F32)
+        numer = tile("numer", [P, len(pieces), 2 * H], F32)
+        moving = ((xg_codes[:].bitcast(U8), xg_plane[:]), (sx_codes[:], sx_plane[:]))
+        for i, (h, r) in enumerate(pieces):
             for s in range(2):
-                est = bank(s * PACK + c, "est%d_%d" % (s, c))
+                est = bank(s * PACK + i, "est%d_%d" % (s, i))
                 codes, plane = moving[s]
-                for t in range(PACK):
-                    cols = slice(s * N + t * M, s * N + (t + 1) * M)
+                for e in range(2):
+                    first = s * N + (2 * r + e) * M
+                    cols = slice(first, first + M)
                     nc.tensor.matmul_mx(
-                        out=est[:, t * C : (t + 1) * C],
+                        out=est[:, e * H : (e + 1) * H],
                         lhsT=w_codes[:, cols].bitcast(FP8X4), lhsT_scale=w_plane[:, cols],
-                        rhs=codes[:, 2 * c * C : 2 * (c + 1) * C].bitcast(FP4X4),
-                        rhs_scale=plane[:, js],
+                        rhs=codes[:, 2 * h * H : 2 * (h + 1) * H].bitcast(FP4X4),
+                        rhs_scale=plane[:, h * H : (h + 1) * H],
                         start=True, stop=True,
                     )
                 nc.vector.tensor_tensor(
-                    terms[:, c, s, :].rearrange("p (t j) -> p t j", t=PACK),
-                    prec[:, s, :, js],
-                    est[:].rearrange("p (t j) -> p t j", t=PACK), ALU.mult,
+                    paired(terms[:, i, s, :]), piece_of(prec[:, s], h, r), paired(est[:]), ALU.mult
                 )
-            adder = nc.vector if c == CHUNKS - 1 else nc.gpsimd
-            adder.tensor_tensor(numer[:, c, :], terms[:, c, 0, :], terms[:, c, 1, :], ALU.add)
+            adder = nc.vector if i == len(pieces) - 1 else nc.gpsimd
+            adder.tensor_tensor(numer[:, i, :], terms[:, i, 0, :], terms[:, i, 1, :], ALU.add)
 
-        recip = tile("recip", [P, CHUNKS, PACK * C], F32)
-        y = tile("y", [P, CHUNKS, PACK * C], F32)
+        recip = tile("recip", [P, PACK, J], F32)
+        y = tile("y", [P, PACK, J], F32)
         y_bf = tile("y_bf", [P, CHUNKS, C * PACK], BF16)
         y_codes = tile("y_codes", [P, J], I32)
         y_plane = tile("y_plane", [P, J], U8)
         out_rows = out_0.rearrange("(p t) j -> p t j", t=PACK)
         for c in range(CHUNKS):
             js = slice(c * C, (c + 1) * C)
-            nc.scalar.activation(
-                recip[:, c, :].rearrange("p (t j) -> p t j", t=PACK),
-                log_total[:, :, js], ACT.Exp, scale=-1.0,
+            nc.scalar.activation(recip[:, :, js], log_total[:, :, js], ACT.Exp, scale=-1.0)
+        for i, (h, r) in enumerate(pieces):
+            nc.vector.tensor_tensor(
+                piece_of(y, h, r), paired(numer[:, i, :]), piece_of(recip, h, r), ALU.mult
             )
-        for c in range(CHUNKS):
-            js = slice(c * C, (c + 1) * C)
-            nc.vector.tensor_tensor(y[:, c, :], numer[:, c, :], recip[:, c, :], ALU.mult)
-            nc.sync.dma_start(
-                out=out_rows[:, :, js], in_=y[:, c, :].rearrange("p (t j) -> p t j", t=PACK)
-            )
-        for c in range(CHUNKS):
-            js = slice(c * C, (c + 1) * C)
-            dst = y_bf[:, c, :].rearrange("p (g i t) -> p g t i", i=4, t=PACK)
-            src = y[:, c, :].rearrange("p (t g i) -> p g t i", i=4, t=PACK)
-            if c < 2:
-                nc.scalar.copy(dst, src)
-            else:
-                nc.vector.tensor_copy(dst, src)
-            nc.vector.quantize_mx(
-                out=y_codes[:, js].bitcast(FP8X4), scales=y_plane[:, js], in_=y_bf[:, c, :]
-            )
+            nc.sync.dma_start(out=piece_of(out_rows, h, r), in_=piece_of(y, h, r))
         for h in range(2):
-            half = slice(h * J // 2, (h + 1) * J // 2)
+            for c in (2 * h, 2 * h + 1):
+                dst = y_bf[:, c, :].rearrange("p (g i t) -> p g t i", i=4, t=PACK)
+                src = y[:, :, c * C : (c + 1) * C].rearrange("p t (g i) -> p g t i", i=4)
+                if c == 2:
+                    nc.vector.tensor_copy(dst, src)
+                else:
+                    nc.scalar.copy(dst, src)
+            half = slice(h * H, (h + 1) * H)
+            nc.vector.quantize_mx(
+                out=y_codes[:, half].bitcast(FP8X4), scales=y_plane[:, half],
+                in_=y_bf[:, 2 * h : 2 * h + 2, :].rearrange("p c w -> p (c w)"),
+            )
             nc.sync.dma_start(out=words_of(out_1)[:, half], in_=y_codes[:, half])
         for q in range(QUADS):
-            nc.scalar.dma_start(
+            (nc.sync, nc.scalar)[q % 2].dma_start(
                 out=out_2[0, 4 * q : 4 * q + 4, :].bitcast(I32),
                 in_=y_plane[32 * q : 32 * q + 4, :].bitcast(I32),
             )

@@ -90,12 +90,12 @@ def tile_list_precision_weighted_pair_pl_kernel(
         vb_codes = tile("vb_codes", [P, 2 * N], U8)
         vb_plane = tile("vb_plane", [P, N], U8)
         nc.vector.tensor_copy(
-            vb_codes[:].rearrange("p (t m b) -> p m t b", t=PACK, b=2),
-            vb_raw[:].rearrange("p (m t b) -> p m t b", t=PACK, b=2),
+            vb_codes[:].rearrange("p (t m b) -> p t m b", t=PACK, b=2),
+            vb_raw[:].rearrange("p (m t b) -> p t m b", t=PACK, b=2),
         )
         nc.vector.tensor_copy(
-            vb_plane[:].rearrange("p (t m) -> p m t", t=PACK),
-            vb_plane_raw[:].rearrange("p (m t) -> p m t", t=PACK),
+            vb_plane[:].rearrange("p (t m) -> p t m", t=PACK),
+            vb_plane_raw[:].rearrange("p (m t) -> p t m", t=PACK),
         )
         for t in range(PACK):
             banks["v", t] = bank(PACK + t, "v%d" % t)
@@ -115,11 +115,11 @@ def tile_list_precision_weighted_pair_pl_kernel(
         nc.vector.tensor_copy(xg_plane[:], xt_plane[:].indirect(offsets[:]))
 
         va_bf = tile("va_bf", [P, PACK, M, PACK], BF16, tag="vb_plane_raw")
-        dealt = va_bf[:].rearrange("p t m j -> p m j t")
-        rows = va_raw[:].rearrange("p j (m t) -> p m j t", t=PACK)
+        dealt = va_bf[:].rearrange("p t m j -> p m t j")
+        rows = va_raw[:].rearrange("p j (m t) -> p m t j", t=PACK)
         nc.scalar.copy(dealt[:, :SCALAR_M], rows[:, :SCALAR_M])
         nc.vector.tensor_copy(dealt[:, SCALAR_M:], rows[:, SCALAR_M:])
-        va_codes = tile("va_codes", [P, N], I32)
+        va_codes = tile("va_codes", [P, N], I32, tag="xt_plane")
         va_plane = tile("va_plane", [P, N], U8)
         for t in range(PACK):
             cols = slice(t * M, (t + 1) * M)
@@ -139,18 +139,19 @@ def tile_list_precision_weighted_pair_pl_kernel(
 
         load_scales(w_plane_raw[:, :N], wa_scales, nc.sync)
         load_scales(w_plane_raw[:, N:], wb_scales, nc.sync)
-        w_codes = tile("w_codes", [P, 2 * N], I32, tag="vb_plane_raw")
-        w_plane = tile("w_plane", [P, 2 * N], U8, tag="va_plane")
+        w_dealt = tile("w_dealt", [P, 2 * N + 2 * N // PACK], I32, tag="va_plane")
+        w_codes = w_dealt[:, : 2 * N]
+        w_plane = w_dealt[:, 2 * N :].bitcast(U8)
         nc.vector.tensor_copy(
-            w_plane[:].rearrange("p (w t m) -> p w m t", w=2, t=PACK),
-            w_plane_raw.rearrange("p (w m t) -> p w m t", w=2, t=PACK),
+            w_plane.rearrange("p (w t m) -> p w t m", w=2, t=PACK),
+            w_plane_raw.rearrange("p (w m t) -> p w t m", w=2, t=PACK),
         )
         nc.vector.tensor_copy(
-            w_codes[:].rearrange("p (w t m) -> p w m t", w=2, t=PACK),
-            w_raw.rearrange("p (w m t) -> p w m t", w=2, t=PACK),
+            w_codes.rearrange("p (w t g i) -> p w g t i", w=2, t=PACK, i=4),
+            w_raw.rearrange("p (w g i t) -> p w g t i", w=2, t=PACK, i=4),
         )
 
-        logs = tile("logs", [P, PACK, 2, J], F32, tag="va_codes")
+        logs = tile("logs", [P, PACK, 2, J], F32, tag="xt_plane")
         prec = tile("prec", [P, 2, PACK, J], F32, tag="w_packed")
         total = tile("total", [P, PACK, J], F32)
         log_total = tile("log_total", [P, PACK, J], F32)
@@ -212,8 +213,8 @@ def tile_list_precision_weighted_pair_pl_kernel(
             nc.sync.dma_start(out=piece_of(out_rows, h, r), in_=piece_of(y, h, r))
         for h in range(2):
             for c in (2 * h, 2 * h + 1):
-                dst = y_bf[:, c, :].rearrange("p (g i t) -> p g t i", i=4, t=PACK)
-                src = y[:, :, c * C : (c + 1) * C].rearrange("p t (g i) -> p g t i", i=4)
+                dst = y_bf[:, c, :].rearrange("p (j t) -> p j t", t=PACK)
+                src = y[:, :, c * C : (c + 1) * C].rearrange("p t j -> p j t")
                 if c == 2:
                     nc.vector.tensor_copy(dst, src)
                 else:

@@ -19,11 +19,12 @@ P = 128
 PACK = 4
 QUADS = 4
 M = N // PACK
-CHUNKS = 4
-C = J // CHUNKS
-H = J // 2
+HALF = J // 2
+LINE = 4
 LINEAR_FROM = 30.0
-SCALAR_M = 40
+FLOOR = 0.1
+SCALAR_PLACES = 40
+SCALAR_SLOTS = 192
 
 
 def tile_list_precision_weighted_pair_pl_kernel(
@@ -38,15 +39,24 @@ def tile_list_precision_weighted_pair_pl_kernel(
         def tile(name, shape, dtype, tag=None):
             return sb.tile(shape, dtype, name=name, tag=tag or name, align_bytes=64)
 
-        def load_scales(plane, scales, queue):
+        def bank(index, name):
+            return ps.tile([P, J], F32, name=name, tag="bank%d" % index)
+
+        def load_scales(plane, scales):
             for q in range(QUADS):
-                queue.dma_start(
+                nc.sync.dma_start(
                     out=plane[32 * q : 32 * q + 4, :].bitcast(I32),
                     in_=scales[0, 4 * q : 4 * q + 4, :].bitcast(I32),
                 )
 
         def words_of(words):
             return words[0].rearrange("p n t -> p (n t)").bitcast(I32)
+
+        def product(out, weight, weight_plane, tokens, token_plane):
+            nc.tensor.matmul_mx(
+                out=out, lhsT=weight, lhsT_scale=weight_plane,
+                rhs=tokens.bitcast(FP4X4), rhs_scale=token_plane, start=True, stop=True,
+            )
 
         offsets = sb.tile([P, J // 16], U16, name="offsets")
         nc.sync.dma_start(offsets[:], offs)
@@ -61,31 +71,20 @@ def tile_list_precision_weighted_pair_pl_kernel(
         sx_plane = tile("sx_plane", [P, J], U8)
         nc.gpsimd.memset(vb_plane_raw[:].bitcast(I32), 0)
         nc.gpsimd.memset(sx_plane[:].bitcast(I32), 0)
-        load_scales(vb_plane_raw, vb_scales, nc.sync)
-        load_scales(sx_plane, sx_scales, nc.sync)
+        load_scales(vb_plane_raw, vb_scales)
+        load_scales(sx_plane, sx_scales)
         va_raw = tile("va_raw", [P, PACK, N], F32)
         nc.gpsimd.dma_start(out=va_raw[:], in_=va.rearrange("(p j) n -> p j n", j=PACK))
 
-        warm = tile("warm", [P, 1], F32)
-        nc.vector.memset(warm[:], 0.0)
-        warm_out = tile("warm_out", [P, 1], F32)
-        nc.scalar.activation(warm_out[:], warm[:], ACT.Exp)
+        zero = tile("zero", [P, 1], F32)
+        nc.vector.memset(zero[:], 0.0)
+        one = tile("one", [P, 1], F32)
+        nc.scalar.activation(one[:], zero[:], ACT.Exp)
         xt_plane = tile("xt_plane", [P, T], U8)
         nc.vector.memset(xt_plane[:].bitcast(I32), 0)
-        load_scales(xt_plane, xt_scales, nc.sync)
+        load_scales(xt_plane, xt_scales)
 
-        w_packed = tile("w_packed", [P, 2 * N + 2 * N // PACK], I32)
-        w_raw = w_packed[:, : 2 * N]
-        nc.gpsimd.memset(w_packed[:, 2 * N :], 0)
-        w_plane_raw = w_packed[:, 2 * N :].bitcast(U8)
-        nc.gpsimd.dma_start(out=w_raw[:, :N], in_=words_of(wa_words))
-        nc.gpsimd.dma_start(out=w_raw[:, N:], in_=words_of(wb_words))
-
-        banks = {}
-
-        def bank(i, name):
-            return ps.tile([P, 512], F32, name=name, tag="bank%d" % i)
-
+        logits = {}
         grown = tile("grown", [P, PACK, 2, J], F32)
         vb_codes = tile("vb_codes", [P, 2 * N], U8)
         vb_plane = tile("vb_plane", [P, N], U8)
@@ -98,16 +97,12 @@ def tile_list_precision_weighted_pair_pl_kernel(
             vb_plane_raw[:].rearrange("p (m t) -> p t m", t=PACK),
         )
         for t in range(PACK):
-            banks["v", t] = bank(PACK + t, "v%d" % t)
-            nc.tensor.matmul_mx(
-                out=banks["v", t][:],
-                lhsT=vb_codes[:, 2 * t * M : 2 * (t + 1) * M].bitcast(FP4X4),
-                lhsT_scale=vb_plane[:, t * M : (t + 1) * M],
-                rhs=sx_codes[:].bitcast(FP4X4), rhs_scale=sx_plane[:],
-                start=True, stop=True,
+            logits["v", t] = bank(PACK + t, "v%d" % t)
+            product(
+                logits["v", t][:], vb_codes[:, 2 * t * M : 2 * (t + 1) * M].bitcast(FP4X4),
+                vb_plane[:, t * M : (t + 1) * M], sx_codes[:], sx_plane[:],
             )
-            nc.scalar.activation(grown[:, t, 1, :], banks["v", t][:], ACT.Exp)
-
+            nc.scalar.activation(grown[:, t, 1, :], logits["v", t][:], ACT.Exp)
 
         xg_plane = tile("xg_plane", [P, J], U8)
         xg_codes = tile("xg_codes", [P, J], U16)
@@ -115,116 +110,113 @@ def tile_list_precision_weighted_pair_pl_kernel(
         nc.vector.tensor_copy(xg_plane[:], xt_plane[:].indirect(offsets[:]))
 
         va_bf = tile("va_bf", [P, PACK, M, PACK], BF16, tag="vb_plane_raw")
-        dealt = va_bf[:].rearrange("p t m j -> p m t j")
-        rows = va_raw[:].rearrange("p j (m t) -> p m t j", t=PACK)
-        nc.scalar.copy(dealt[:, :SCALAR_M], rows[:, :SCALAR_M])
-        nc.vector.tensor_copy(dealt[:, SCALAR_M:], rows[:, SCALAR_M:])
+        va_dealt = va_bf[:].rearrange("p t m j -> p m t j")
+        va_rows = va_raw[:].rearrange("p j (m t) -> p m t j", t=PACK)
+        nc.scalar.copy(va_dealt[:, :SCALAR_PLACES], va_rows[:, :SCALAR_PLACES])
+        nc.vector.tensor_copy(va_dealt[:, SCALAR_PLACES:], va_rows[:, SCALAR_PLACES:])
         va_codes = tile("va_codes", [P, N], I32, tag="xt_plane")
         va_plane = tile("va_plane", [P, N], U8)
         for t in range(PACK):
-            cols = slice(t * M, (t + 1) * M)
+            places = slice(t * M, (t + 1) * M)
             nc.vector.quantize_mx(
-                out=va_codes[:, cols].bitcast(FP8X4),
-                scales=va_plane[:, cols],
+                out=va_codes[:, places].bitcast(FP8X4),
+                scales=va_plane[:, places],
                 in_=va_bf[:, t, :, :].rearrange("p m j -> p (m j)"),
             )
-            banks["u", t] = bank(t, "u%d" % t)
-            nc.tensor.matmul_mx(
-                out=banks["u", t][:],
-                lhsT=va_codes[:, cols].bitcast(FP8X4), lhsT_scale=va_plane[:, cols],
-                rhs=xg_codes[:].bitcast(FP4X4), rhs_scale=xg_plane[:],
-                start=True, stop=True,
+            logits["u", t] = bank(t, "u%d" % t)
+            product(
+                logits["u", t][:], va_codes[:, places].bitcast(FP8X4), va_plane[:, places],
+                xg_codes[:], xg_plane[:],
             )
-            nc.scalar.activation(grown[:, t, 0, :], banks["u", t][:], ACT.Exp)
+            nc.scalar.activation(grown[:, t, 0, :], logits["u", t][:], ACT.Exp)
 
-        load_scales(w_plane_raw[:, :N], wa_scales, nc.sync)
-        load_scales(w_plane_raw[:, N:], wb_scales, nc.sync)
+        w_packed = tile("w_packed", [P, 2 * N + 2 * N // PACK], I32, tag="xt_table")
+        w_raw = w_packed[:, : 2 * N]
+        nc.sync.dma_start(out=w_raw[:, :N], in_=words_of(wa_words))
+        nc.sync.dma_start(out=w_raw[:, N:], in_=words_of(wb_words))
+        nc.vector.memset(w_packed[:, 2 * N :], 0)
+        w_plane_raw = w_packed[:, 2 * N :].bitcast(U8)
+        load_scales(w_plane_raw[:, :N], wa_scales)
+        load_scales(w_plane_raw[:, N:], wb_scales)
         w_dealt = tile("w_dealt", [P, 2 * N + 2 * N // PACK], I32, tag="va_plane")
         w_codes = w_dealt[:, : 2 * N]
         w_plane = w_dealt[:, 2 * N :].bitcast(U8)
         nc.vector.tensor_copy(
+            w_codes.rearrange("p (w t g i) -> p w g t i", w=2, t=PACK, i=LINE),
+            w_raw.rearrange("p (w g i t) -> p w g t i", w=2, t=PACK, i=LINE),
+        )
+        nc.vector.tensor_copy(
             w_plane.rearrange("p (w t m) -> p w t m", w=2, t=PACK),
             w_plane_raw.rearrange("p (w m t) -> p w t m", w=2, t=PACK),
         )
-        nc.vector.tensor_copy(
-            w_codes.rearrange("p (w t g i) -> p w g t i", w=2, t=PACK, i=4),
-            w_raw.rearrange("p (w g i t) -> p w g t i", w=2, t=PACK, i=4),
-        )
 
         logs = tile("logs", [P, PACK, 2, J], F32, tag="xt_plane")
-        prec = tile("prec", [P, 2, PACK, J], F32, tag="w_packed")
+        prec = tile("prec", [P, 2, PACK, J], F32, tag="xt_table")
         total = tile("total", [P, PACK, J], F32)
         log_total = tile("log_total", [P, PACK, J], F32)
         for t in range(PACK):
             for s, side in enumerate("uv"):
-                nc.scalar.activation(logs[:, t, s, :], grown[:, t, s, :], ACT.Ln, bias=1.0)
+                nc.scalar.activation(logs[:, t, s, :], grown[:, t, s, :], ACT.Ln, bias=one[:])
                 nc.vector.scalar_tensor_tensor(
-                    prec[:, s, t, :], logs[:, t, s, :], LINEAR_FROM, banks[side, t][:],
+                    prec[:, s, t, :], logs[:, t, s, :], LINEAR_FROM, logits[side, t][:],
                     ALU.min, ALU.max,
                 )
             nc.gpsimd.tensor_tensor(total[:, t, :], prec[:, 0, t, :], prec[:, 1, t, :], ALU.add)
         for t in range(PACK):
-            nc.scalar.activation(log_total[:, t, :], total[:, t, :], ACT.Ln, bias=0.1)
+            nc.scalar.activation(log_total[:, t, :], total[:, t, :], ACT.Ln, bias=FLOOR)
 
-        pieces = [(h, r) for h in range(2) for r in range(2)]
+        terms = tile("terms", [P, PACK, 2, J], F32)
+        numer = tile("numer", [P, PACK, J], F32)
+        moving = ((xg_codes[:], xg_plane[:]), (sx_codes[:], sx_plane[:]))
+        last = PACK - 1
 
-        def piece_of(whole, h, r):
-            return whole[:, 2 * r : 2 * r + 2, h * H : (h + 1) * H]
+        def add_terms(engine, t):
+            engine.tensor_tensor(numer[:, t, :], terms[:, t, 0, :], terms[:, t, 1, :], ALU.add)
 
-        def paired(flat):
-            return flat.rearrange("p (t j) -> p t j", t=2)
-
-        terms = tile("terms", [P, len(pieces), 2, 2 * H], F32)
-        numer = tile("numer", [P, len(pieces), 2 * H], F32)
-        moving = ((xg_codes[:].bitcast(U8), xg_plane[:]), (sx_codes[:], sx_plane[:]))
-        for i, (h, r) in enumerate(pieces):
+        for t in range(PACK):
             for s in range(2):
-                est = bank(s * PACK + i, "est%d_%d" % (s, i))
-                codes, plane = moving[s]
-                for e in range(2):
-                    first = s * N + (2 * r + e) * M
-                    cols = slice(first, first + M)
-                    nc.tensor.matmul_mx(
-                        out=est[:, e * H : (e + 1) * H],
-                        lhsT=w_codes[:, cols].bitcast(FP8X4), lhsT_scale=w_plane[:, cols],
-                        rhs=codes[:, 2 * h * H : 2 * (h + 1) * H].bitcast(FP4X4),
-                        rhs_scale=plane[:, h * H : (h + 1) * H],
-                        start=True, stop=True,
-                    )
-                nc.vector.tensor_tensor(
-                    paired(terms[:, i, s, :]), piece_of(prec[:, s], h, r), paired(est[:]), ALU.mult
+                estimate = bank(s * PACK + t, "estimate%d_%d" % (s, t))
+                places = slice(s * N + t * M, s * N + (t + 1) * M)
+                product(
+                    estimate[:], w_codes[:, places].bitcast(FP8X4), w_plane[:, places], *moving[s]
                 )
-            adder = nc.vector if i == len(pieces) - 1 else nc.gpsimd
-            adder.tensor_tensor(numer[:, i, :], terms[:, i, 0, :], terms[:, i, 1, :], ALU.add)
+                nc.vector.tensor_tensor(terms[:, t, s, :], prec[:, s, t, :], estimate[:], ALU.mult)
+            if t < last:
+                add_terms(nc.gpsimd, t)
 
-        recip = tile("recip", [P, PACK, J], F32)
+        recip = tile("recip", [P, PACK, J], F32, tag="total")
         y = tile("y", [P, PACK, J], F32)
-        y_bf = tile("y_bf", [P, CHUNKS, C * PACK], BF16)
+        out_rows = out_0.rearrange("(p t) j -> p t j", t=PACK)
+        for t in range(PACK):
+            nc.scalar.activation(recip[:, t, :], log_total[:, t, :], ACT.Exp, scale=-1.0)
+        for t in range(PACK):
+            if t == last - 1:
+                add_terms(nc.vector, last)
+            nc.vector.tensor_tensor(y[:, t, :], numer[:, t, :], recip[:, t, :], ALU.mult)
+            nc.sync.dma_start(out=out_rows[:, t, :], in_=y[:, t, :])
+
+        y_bf = tile("y_bf", [P, J * PACK], BF16)
         y_codes = tile("y_codes", [P, J], I32)
         y_plane = tile("y_plane", [P, J], U8)
-        out_rows = out_0.rearrange("(p t) j -> p t j", t=PACK)
-        for c in range(CHUNKS):
-            js = slice(c * C, (c + 1) * C)
-            nc.scalar.activation(recip[:, :, js], log_total[:, :, js], ACT.Exp, scale=-1.0)
-        for i, (h, r) in enumerate(pieces):
-            nc.vector.tensor_tensor(
-                piece_of(y, h, r), paired(numer[:, i, :]), piece_of(recip, h, r), ALU.mult
+
+        def round_slots(copy, first, end):
+            copy(
+                y_bf[:, first * PACK : end * PACK].rearrange(
+                    "p (g i t) -> p g t i", i=LINE, t=PACK
+                ),
+                y[:, :, first:end].rearrange("p t (g i) -> p g t i", i=LINE),
             )
-            nc.sync.dma_start(out=piece_of(out_rows, h, r), in_=piece_of(y, h, r))
-        for h in range(2):
-            for c in (2 * h, 2 * h + 1):
-                dst = y_bf[:, c, :].rearrange("p (j t) -> p j t", t=PACK)
-                src = y[:, :, c * C : (c + 1) * C].rearrange("p t j -> p j t")
-                if c == 2:
-                    nc.vector.tensor_copy(dst, src)
-                else:
-                    nc.scalar.copy(dst, src)
-            half = slice(h * H, (h + 1) * H)
+
+        round_slots(nc.vector.tensor_copy, 0, HALF)
+        round_slots(nc.vector.tensor_copy, HALF, J - SCALAR_SLOTS)
+        round_slots(nc.scalar.copy, J - SCALAR_SLOTS, J)
+        for first in (0, HALF):
+            slots = slice(first, first + HALF)
             nc.vector.quantize_mx(
-                out=y_codes[:, half].bitcast(FP8X4), scales=y_plane[:, half],
-                in_=y_bf[:, 2 * h : 2 * h + 2, :].rearrange("p c w -> p (c w)"),
+                out=y_codes[:, slots].bitcast(FP8X4), scales=y_plane[:, slots],
+                in_=y_bf[:, first * PACK : (first + HALF) * PACK],
             )
-            nc.sync.dma_start(out=words_of(out_1)[:, half], in_=y_codes[:, half])
+            nc.sync.dma_start(out=words_of(out_1)[:, slots], in_=y_codes[:, slots])
         for q in range(QUADS):
             (nc.sync, nc.scalar)[q % 2].dma_start(
                 out=out_2[0, 4 * q : 4 * q + 4, :].bitcast(I32),

from contextlib import ExitStack

import concourse.mybir as mybir

K, T, J, N = 512, 2048, 512, 512
FLOPS = 4 * 2 * K * J * N

F32 = mybir.dt.float32
BF16 = mybir.dt.bfloat16
I32 = mybir.dt.int32
U16 = mybir.dt.uint16
U8 = mybir.dt.uint8
FP8X4 = mybir.dt.float8_e4m3fn_x4
FP4X4 = mybir.dt.float4_e2m1fn_x4
ALU = mybir.AluOpType
ACT = mybir.ActivationFunctionType

P = 128
PACK = 4
QUADS = 4
M = N // PACK
HALF = J // 2
LINE = 4
LINEAR_FROM = 30.0
FLOOR = 0.1
SCALAR_PLACES = 40
SCALAR_SLOTS = 192


def tile_list_precision_weighted_pair_pl_kernel(
    tc, xt_words, xt_scales, wa_words, wa_scales, va, sx_words, sx_scales,
    wb_words, wb_scales, vb_words, vb_scales, offs, out_0, out_1, out_2,
):
    nc = tc.nc
    with ExitStack() as ctx:
        sb = ctx.enter_context(tc.tile_pool(name="sb", bufs=1))
        ps = ctx.enter_context(tc.psum_pool(name="ps", bufs=1))

        def tile(name, shape, dtype, tag=None):
            return sb.tile(shape, dtype, name=name, tag=tag or name, align_bytes=64)

        def bank(index, name):
            return ps.tile([P, J], F32, name=name, tag="bank%d" % index)

        def load_scales(plane, scales):
            for q in range(QUADS):
                nc.sync.dma_start(
                    out=plane[32 * q : 32 * q + 4, :].bitcast(I32),
                    in_=scales[0, 4 * q : 4 * q + 4, :].bitcast(I32),
                )

        def words_of(words):
            return words[0].rearrange("p n t -> p (n t)").bitcast(I32)

        def product(out, weight, weight_plane, tokens, token_plane):
            nc.tensor.matmul_mx(
                out=out, lhsT=weight, lhsT_scale=weight_plane,
                rhs=tokens.bitcast(FP4X4), rhs_scale=token_plane, start=True, stop=True,
            )

        offsets = sb.tile([P, J // 16], U16, name="offsets")
        nc.sync.dma_start(offsets[:], offs)
        xt_table = tile("xt_table", [P, T], U16)
        nc.sync.dma_start(out=xt_table[:].bitcast(I32), in_=xt_words[0].bitcast(I32))
        sx_codes = tile("sx_codes", [P, 2 * J], U8)
        vb_raw = tile("vb_raw", [P, 2 * N], U8)
        nc.sync.dma_start(out=vb_raw[:].bitcast(I32), in_=vb_words[0].bitcast(I32))
        nc.sync.dma_start(out=sx_codes[:].bitcast(I32), in_=sx_words[0].bitcast(I32))

        vb_plane_raw = tile("vb_plane_raw", [P, N], U8)
        sx_plane = tile("sx_plane", [P, J], U8)
        nc.gpsimd.memset(vb_plane_raw[:].bitcast(I32), 0)
        nc.gpsimd.memset(sx_plane[:].bitcast(I32), 0)
        load_scales(vb_plane_raw, vb_scales)
        load_scales(sx_plane, sx_scales)
        va_raw = tile("va_raw", [P, PACK, N], F32)
        nc.gpsimd.dma_start(out=va_raw[:], in_=va.rearrange("(p j) n -> p j n", j=PACK))

        zero = tile("zero", [P, 1], F32)
        nc.vector.memset(zero[:], 0.0)
        one = tile("one", [P, 1], F32)
        nc.scalar.activation(one[:], zero[:], ACT.Exp)
        xt_plane = tile("xt_plane", [P, T], U8)
        nc.vector.memset(xt_plane[:].bitcast(I32), 0)
        load_scales(xt_plane, xt_scales)

        logits = {}
        grown = tile("grown", [P, PACK, 2, J], F32)
        vb_codes = tile("vb_codes", [P, 2 * N], U8)
        vb_plane = tile("vb_plane", [P, N], U8)
        nc.vector.tensor_copy(
            vb_codes[:].rearrange("p (t m b) -> p t m b", t=PACK, b=2),
            vb_raw[:].rearrange("p (m t b) -> p t m b", t=PACK, b=2),
        )
        nc.vector.tensor_copy(
            vb_plane[:].rearrange("p (t m) -> p t m", t=PACK),
            vb_plane_raw[:].rearrange("p (m t) -> p t m", t=PACK),
        )
        for t in range(PACK):
            logits["v", t] = bank(PACK + t, "v%d" % t)
            product(
                logits["v", t][:], vb_codes[:, 2 * t * M : 2 * (t + 1) * M].bitcast(FP4X4),
                vb_plane[:, t * M : (t + 1) * M], sx_codes[:], sx_plane[:],
            )
            nc.scalar.activation(grown[:, t, 1, :], logits["v", t][:], ACT.Exp)

        xg_plane = tile("xg_plane", [P, J], U8)
        xg_codes = tile("xg_codes", [P, J], U16)
        nc.vector.tensor_copy(xg_codes[:], xt_table[:].indirect(offsets[:]))
        nc.vector.tensor_copy(xg_plane[:], xt_plane[:].indirect(offsets[:]))

        va_bf = tile("va_bf", [P, PACK, M, PACK], BF16, tag="vb_plane_raw")
        va_dealt = va_bf[:].rearrange("p t m j -> p m t j")
        va_rows = va_raw[:].rearrange("p j (m t) -> p m t j", t=PACK)
        nc.scalar.copy(va_dealt[:, :SCALAR_PLACES], va_rows[:, :SCALAR_PLACES])
        nc.vector.tensor_copy(va_dealt[:, SCALAR_PLACES:], va_rows[:, SCALAR_PLACES:])
        va_codes = tile("va_codes", [P, N], I32, tag="xt_plane")
        va_plane = tile("va_plane", [P, N], U8)
        for t in range(PACK):
            places = slice(t * M, (t + 1) * M)
            nc.vector.quantize_mx(
                out=va_codes[:, places].bitcast(FP8X4),
                scales=va_plane[:, places],
                in_=va_bf[:, t, :, :].rearrange("p m j -> p (m j)"),
            )
            logits["u", t] = bank(t, "u%d" % t)
            product(
                logits["u", t][:], va_codes[:, places].bitcast(FP8X4), va_plane[:, places],
                xg_codes[:], xg_plane[:],
            )
            nc.scalar.activation(grown[:, t, 0, :], logits["u", t][:], ACT.Exp)

        w_packed = tile("w_packed", [P, 2 * N + 2 * N // PACK], I32, tag="xt_table")
        w_raw = w_packed[:, : 2 * N]
        nc.sync.dma_start(out=w_raw[:, :N], in_=words_of(wa_words))
        nc.sync.dma_start(out=w_raw[:, N:], in_=words_of(wb_words))
        nc.vector.memset(w_packed[:, 2 * N :], 0)
        w_plane_raw = w_packed[:, 2 * N :].bitcast(U8)
        load_scales(w_plane_raw[:, :N], wa_scales)
        load_scales(w_plane_raw[:, N:], wb_scales)
        w_dealt = tile("w_dealt", [P, 2 * N + 2 * N // PACK], I32, tag="va_plane")
        w_codes = w_dealt[:, : 2 * N]
        w_plane = w_dealt[:, 2 * N :].bitcast(U8)
        nc.vector.tensor_copy(
            w_codes.rearrange("p (w t g i) -> p w g t i", w=2, t=PACK, i=LINE),
            w_raw.rearrange("p (w g i t) -> p w g t i", w=2, t=PACK, i=LINE),
        )
        nc.vector.tensor_copy(
            w_plane.rearrange("p (w t m) -> p w t m", w=2, t=PACK),
            w_plane_raw.rearrange("p (w m t) -> p w t m", w=2, t=PACK),
        )

        logs = tile("logs", [P, PACK, 2, J], F32, tag="xt_plane")
        prec = tile("prec", [P, 2, PACK, J], F32, tag="xt_table")
        total = tile("total", [P, PACK, J], F32)
        log_total = tile("log_total", [P, PACK, J], F32)
        for t in range(PACK):
            for s, side in enumerate("uv"):
                nc.scalar.activation(logs[:, t, s, :], grown[:, t, s, :], ACT.Ln, bias=one[:])
                nc.vector.scalar_tensor_tensor(
                    prec[:, s, t, :], logs[:, t, s, :], LINEAR_FROM, logits[side, t][:],
                    ALU.min, ALU.max,
                )
            nc.gpsimd.tensor_tensor(total[:, t, :], prec[:, 0, t, :], prec[:, 1, t, :], ALU.add)
        for t in range(PACK):
            nc.scalar.activation(log_total[:, t, :], total[:, t, :], ACT.Ln, bias=FLOOR)

        terms = tile("terms", [P, PACK, 2, J], F32)
        numer = tile("numer", [P, PACK, J], F32)
        moving = ((xg_codes[:], xg_plane[:]), (sx_codes[:], sx_plane[:]))
        last = PACK - 1

        def add_terms(engine, t):
            engine.tensor_tensor(numer[:, t, :], terms[:, t, 0, :], terms[:, t, 1, :], ALU.add)

        for t in range(PACK):
            for s in range(2):
                estimate = bank(s * PACK + t, "estimate%d_%d" % (s, t))
                places = slice(s * N + t * M, s * N + (t + 1) * M)
                product(
                    estimate[:], w_codes[:, places].bitcast(FP8X4), w_plane[:, places], *moving[s]
                )
                nc.vector.tensor_tensor(terms[:, t, s, :], prec[:, s, t, :], estimate[:], ALU.mult)
            if t < last:
                add_terms(nc.gpsimd, t)

        recip = tile("recip", [P, PACK, J], F32, tag="total")
        y = tile("y", [P, PACK, J], F32)
        out_rows = out_0.rearrange("(p t) j -> p t j", t=PACK)
        for t in range(PACK):
            nc.scalar.activation(recip[:, t, :], log_total[:, t, :], ACT.Exp, scale=-1.0)
        for t in range(PACK):
            if t == last - 1:
                add_terms(nc.vector, last)
            nc.vector.tensor_tensor(y[:, t, :], numer[:, t, :], recip[:, t, :], ALU.mult)
            nc.sync.dma_start(out=out_rows[:, t, :], in_=y[:, t, :])

        y_bf = tile("y_bf", [P, J * PACK], BF16)
        y_codes = tile("y_codes", [P, J], I32)
        y_plane = tile("y_plane", [P, J], U8)

        def round_slots(copy, first, end):
            copy(
                y_bf[:, first * PACK : end * PACK].rearrange(
                    "p (g i t) -> p g t i", i=LINE, t=PACK
                ),
                y[:, :, first:end].rearrange("p t (g i) -> p g t i", i=LINE),
            )

        round_slots(nc.vector.tensor_copy, 0, HALF)
        round_slots(nc.vector.tensor_copy, HALF, J - SCALAR_SLOTS)
        round_slots(nc.scalar.copy, J - SCALAR_SLOTS, J)
        for first in (0, HALF):
            slots = slice(first, first + HALF)
            nc.vector.quantize_mx(
                out=y_codes[:, slots].bitcast(FP8X4), scales=y_plane[:, slots],
                in_=y_bf[:, first * PACK : (first + HALF) * PACK],
            )
            nc.sync.dma_start(out=words_of(out_1)[:, slots], in_=y_codes[:, slots])
        for q in range(QUADS):
            (nc.sync, nc.scalar)[q % 2].dma_start(
                out=out_2[0, 4 * q : 4 * q + 4, :].bitcast(I32),
                in_=y_plane[32 * q : 32 * q + 4, :].bitcast(I32),
            )
